import numpy as np
import ml_dtypes


def mxq(x, axis, fmt="e4m3"):
    dtype, down = {"e4m3": (ml_dtypes.float8_e4m3fn, 7), "e5m2": (ml_dtypes.float8_e5m2, 14)}[fmt]
    v = np.moveaxis(np.asarray(x, np.float32).astype(ml_dtypes.bfloat16).astype(np.float64), axis, -1)
    blocks = v.reshape(v.shape[:-1] + (-1, 32))
    amax = np.abs(blocks).max(-1, keepdims=True)
    byte = np.maximum(np.where(amax > 0, np.frexp(amax)[1] - 1 + 127, 0) - down, 1)
    scale = np.exp2(byte - 127.0)
    codes = (blocks / scale).astype(np.float32).astype(dtype).astype(np.float64)
    return np.moveaxis((codes * scale).reshape(v.shape), -1, axis)


WIDE = False


def mx_kscale(k):
    if not WIDE:
        return np.ones(k)
    levels = np.array([10, -10, 5, -5, 0])
    if k % 512:
        return np.exp2(np.random.permutation(np.resize(levels, k // 32))).repeat(32)
    a = np.empty((k // 512, 16))
    for p in range(k // 512):
        a[p, :8] = np.random.permutation(np.resize(levels, 8))
        for g in range(8):
            far = levels[np.abs(levels - a[p, g]) >= 10]
            a[p, g + 8] = far[np.random.randint(len(far))]
    return np.exp2(a.ravel()).repeat(32)


def f64(x):
    return np.asarray(x).astype(np.float64)


def striped8(idx):
    return np.concatenate([x.reshape(-1, 16).T for x in idx]).astype(np.uint16)


def runs(offs, k):
    lists = np.stack([offs[16 * r : 16 * r + 16].T.reshape(-1) for r in range(8)]).astype(np.int64)
    return lists[np.arange(k) % 512 // 64]


def pack_weight(w):
    k, n = w.shape
    w = f64(np.asarray(w, np.float32).astype(ml_dtypes.bfloat16)).reshape(k // 32, 32, n)
    amax = np.abs(w).max(1)
    byte = np.clip(np.where(amax > 0, np.frexp(amax)[1] - 1 + 127 - 7, 1), 1, 254)
    scaled = (w * np.exp2(127.0 - byte)[:, None, :]).reshape(k, n).astype(np.float32)
    words = np.ascontiguousarray(scaled.reshape(k // 512, 128, 4, n).transpose(0, 1, 3, 2)).astype(ml_dtypes.float8_e4m3fn).view(np.uint8)
    return words, np.ascontiguousarray(byte.astype(np.uint8).reshape(k // 512, 16, n))


def unpack_weight(words, scales):
    g, p, n, _ = words.shape
    vals = np.ascontiguousarray(words).view(ml_dtypes.float8_e4m3fn).astype(np.float64) * np.repeat(np.exp2(scales.astype(np.float64) - 127.0), 8, axis=1)[..., None]
    return vals.transpose(0, 1, 3, 2).reshape(g * 512, n)


def sigmoid(v):
    return 1.0 / (1.0 + np.exp(-np.maximum(v, -700.0)))


K, T, S, N, H, W = 512, 2048, 512, 512, 512, 256


def setup_inputs():
    n = np.random.standard_normal
    s = mx_kscale(K)[:, None]
    u = mx_kscale(H)
    packed_xT = pack_weight(n((K, T)) * s)
    perm = np.stack([np.random.permutation(S) for _ in range(8)])
    return {
        "x_words": packed_xT[0],
        "x_scales": packed_xT[1],
        "w1": (n((K, H)) / np.sqrt(K) / s).astype(np.float32),
        "gn": (np.random.uniform(0.5, 1.5, (H, 1)) * u[:, None]).astype(np.float32),
        "w2": (n((H, N)) / np.sqrt(H) / u[:, None]).astype(np.float32),
        "offs": striped8(np.random.randint(0, T, (8, S))),
        "n1": striped8(perm[:, :W]),
        "n2": striped8(perm[:, W:]),
        "n3": striped8(np.stack([np.random.permutation(S) for _ in range(8)])),
    }


def reference(x_words, x_scales, w1, gn, w2, offs, n1, n2, n3):
    xq = unpack_weight(x_words, x_scales)[np.arange(K)[:, None], runs(offs, K)]
    y = mxq(f64(w1), 0, "e4m3").T @ xq
    pa = y[np.arange(H)[:, None], runs(n1, H)]
    pb = y[np.arange(H)[:, None], runs(n2, H)]
    ra = np.maximum(pa, pb)
    ds = y.copy()
    ds[np.arange(H)[:, None], runs(n1, H)] = ra
    z = f64(gn) * ds
    h = mxq(f64(w2), 0, "e4m3").T @ mxq(z, 0, "e4m3")
    return h * (sigmoid(h[np.arange(N)[:, None], runs(n3, N)]))

@@ -1,0 +1,198 @@
+from contextlib import ExitStack
+
+import concourse.mybir as mybir
+
+K, T, S, H, N, W = 512, 2048, 512, 512, 512, 256
+FLOPS = 2 * K * H * S + 2 * H * N * S
+
+F32 = mybir.dt.float32
+BF16 = mybir.dt.bfloat16
+I32 = mybir.dt.int32
+U32 = mybir.dt.uint32
+U16 = mybir.dt.uint16
+U8 = mybir.dt.uint8
+FP8X4 = mybir.dt.float8_e4m3fn_x4
+ALU = mybir.AluOpType
+ACT = mybir.ActivationFunctionType
+
+P = 128
+PACK = 4
+HALF = 256
+W1_SCALAR_COLS = 96
+VECTOR_GATHERS = (0,)
+
+
+def load_weight(nc, pool, w):
+    rows = w.rearrange("(p j) c -> p j c", j=PACK)
+    halves = []
+    for n in range(2):
+        raw = pool.tile([P, PACK, HALF], F32, name="raw%d" % n)
+        nc.sync.dma_start(out=raw[:], in_=rows[:, :, n * HALF : (n + 1) * HALF])
+        halves.append(raw)
+    return halves
+
+
+def round_and_deal(copy, grouped, halves, c0, c1):
+    raw = halves[c0 // HALF][:, :, c0 % HALF : (c1 - 1) % HALF + 1]
+    m = slice(c0 // PACK, c1 // PACK)
+    copy(grouped[:, :, m, :].rearrange("p t m j -> p m j t"), raw.rearrange("p j (m t) -> p m j t", t=PACK))
+
+
+def tile_picked_hashfillgate_none_p_kernel(tc, x_words, x_scales, w1, gn, w2, offs, n1, n2, n3, out):
+    nc = tc.nc
+    with ExitStack() as ctx:
+        keep = ctx.enter_context(tc.tile_pool(name="keep", bufs=1))
+        stage = ctx.enter_context(tc.tile_pool(name="stage", bufs=1))
+        psum = ctx.enter_context(tc.psum_pool(name="psum", bufs=1))
+
+        scale_table = stage.tile([P, T], U8, align_bytes=64, tag="x_side")
+        nc.vector.memset(scale_table[:].bitcast(I32), 0)
+        warm = keep.tile([P, 8], F32)
+        nc.vector.memset(warm[:], 0.0)
+        offs_sb = keep.tile([P, S // 16], U16)
+        nc.sync.dma_start(offs_sb[:], offs)
+        warm_out = keep.tile([P, 8], F32)
+        nc.scalar.activation(warm_out[:], warm[:], ACT.Sigmoid)
+
+        n1_sb = keep.tile([P, W // 16], U16)
+        nc.sync.dma_start(n1_sb[:], n1)
+        n2_sb = keep.tile([P, W // 16], U16)
+        nc.sync.dma_start(n2_sb[:], n2)
+        n3_sb = keep.tile([P, S // 16], U16)
+        nc.sync.dma_start(n3_sb[:], n3)
+        gain = keep.tile([P, PACK], F32)
+        nc.sync.dma_start(out=gain[:], in_=gn.rearrange("(p t) o -> p (t o)", t=PACK))
+        scale_rows = x_scales[0].bitcast(I32)
+        for e in range(2):
+            nc.sync.dma_start(out=scale_table[:].bitcast(I32)[e:P:16, :], in_=scale_rows[e:16:2, :])
+        word_table = keep.tile([P, T], U32, align_bytes=64)
+        nc.sync.dma_start(out=word_table[:].bitcast(I32), in_=x_words[0].rearrange("p n t -> p (n t)").bitcast(I32))
+        w1_halves = load_weight(nc, stage, w1)
+
+        picked_scales = keep.tile([P, S], U8, align_bytes=64)
+        nc.vector.tensor_copy(picked_scales[:], scale_table[:].indirect(offs_sb[:]))
+        x_plane = keep.tile([P, S], U8, align_bytes=64)
+        nc.vector.tensor_copy(x_plane[:].bitcast(I32), picked_scales[:].bitcast(I32))
+        for e in range(2):
+            nc.scalar.dma_start(out=x_plane[:].bitcast(I32)[2 + e : P : 32, :], in_=picked_scales[:].bitcast(I32)[16 + e : P : 32, :])
+        x_codes = stage.tile([P, S], U32, align_bytes=64, tag="x_side")
+        nc.vector.tensor_copy(x_codes[:], word_table[:].indirect(offs_sb[:]))
+
+        w1_grouped = keep.tile([P, PACK, P, PACK], BF16, align_bytes=64)
+        round_and_deal(nc.vector.tensor_copy, w1_grouped, w1_halves, 0, HALF)
+        round_and_deal(nc.vector.tensor_copy, w1_grouped, w1_halves, HALF, H - W1_SCALAR_COLS)
+        round_and_deal(nc.scalar.copy, w1_grouped, w1_halves, H - W1_SCALAR_COLS, H)
+        w1_codes = keep.tile([P, H], U32, align_bytes=64)
+        w1_plane = keep.tile([P, H], U8, align_bytes=64)
+        order = (1, 0, 3, 2)
+        y_psum = {}
+        for t in order:
+            cols = slice(t * P, (t + 1) * P)
+            nc.vector.quantize_mx(
+                out=w1_codes[:, cols].bitcast(FP8X4),
+                scales=w1_plane[:, cols],
+                in_=w1_grouped[:, t, :, :].rearrange("p m j -> p (m j)"),
+            )
+            y_psum[t] = psum.tile([P, S], F32, name="y_psum%d" % t)
+            nc.tensor.matmul_mx(
+                out=y_psum[t][:],
+                lhsT=w1_codes[:, cols].bitcast(FP8X4),
+                lhsT_scale=w1_plane[:, cols],
+                rhs=x_codes[:].bitcast(FP8X4),
+                rhs_scale=x_plane[:],
+                start=True,
+                stop=True,
+            )
+
+        y = {}
+        for t in order:
+            y[t] = keep.tile([P, S], F32, name="y%d" % t)
+            nc.scalar.copy(y[t][:], y_psum[t][:])
+
+        last, mate = order[3], order[2]
+        z_pair = keep.tile([P, 2 * S], F32)
+        nc.scalar.activation(z_pair[:, :S], y_psum[last][:], ACT.Copy, scale=gain[:, last : last + 1])
+        gain_wide = keep.tile([P, W], F32)
+        nc.scalar.activation(gain_wide[:], gain[:, last : last + 1].to_broadcast([P, W]), ACT.Copy)
+
+        w2_halves = load_weight(nc, stage, w2)
+        w2_grouped = keep.tile([P, PACK, P, PACK], BF16, align_bytes=64)
+        w2_codes = keep.tile([P, N], U32, align_bytes=64)
+        w2_plane = keep.tile([P, N], U8, align_bytes=64)
+        for n in range(2):
+            round_and_deal(nc.scalar.copy, w2_grouped, w2_halves, n * HALF, (n + 1) * HALF)
+        nc.vector.quantize_mx(
+            out=w2_codes[:].bitcast(FP8X4),
+            scales=w2_plane[:],
+            in_=w2_grouped[:].rearrange("p t m j -> p (t m j)"),
+        )
+
+        z_grouped = keep.tile([P, S, PACK], BF16, align_bytes=64)
+        for t in order:
+            pa = keep.tile([P, W], F32, name="pa%d" % t)
+            pb = keep.tile([P, W], F32, name="pb%d" % t)
+            ra = keep.tile([P, W], F32, name="ra%d" % t)
+            nc.vector.tensor_copy(pa[:], y[t][:].indirect(n1_sb[:]))
+            nc.vector.tensor_copy(pb[:], y[t][:].indirect(n2_sb[:]))
+            nc.vector.tensor_tensor(ra[:], pa[:], pb[:], ALU.max)
+            if t == last:
+                nc.vector.tensor_tensor(z_pair[:].indirect(n1_sb[:]), ra[:], gain_wide[:], ALU.mult)
+            else:
+                nc.vector.tensor_copy(y[t][:].indirect(n1_sb[:]), ra[:])
+                dst = z_pair[:, S:] if t == mate else z_grouped[:, :, t]
+                nc.scalar.activation(dst, y[t][:], ACT.Copy, scale=gain[:, t : t + 1])
+
+        src = z_pair[:].rearrange("p (e c) -> p c e", e=2)
+        z_codes = keep.tile([P, S], U32, align_bytes=64)
+        z_plane = keep.tile([P, S], U8, align_bytes=64)
+        for half, copy in enumerate((nc.vector.tensor_copy, nc.scalar.copy)):
+            places = slice(half * HALF, (half + 1) * HALF)
+            copy(z_grouped[:, places, last : mate + 1], src[:, places, :])
+        for half in range(2):
+            places = slice(half * HALF, (half + 1) * HALF)
+            nc.vector.quantize_mx(
+                out=z_codes[:, places].bitcast(FP8X4),
+                scales=z_plane[:, places],
+                in_=z_grouped[:, places, :].rearrange("p c t -> p (c t)"),
+            )
+
+        h_psum = []
+        for t in range(PACK):
+            cols = slice(t * P, (t + 1) * P)
+            bank = psum.tile([P, S], F32, name="h_psum%d" % t)
+            h_psum.append(bank)
+            for half in range(2):
+                places = slice(half * HALF, (half + 1) * HALF)
+                nc.tensor.matmul_mx(
+                    out=bank[:, places],
+                    lhsT=w2_codes[:, cols].bitcast(FP8X4),
+                    lhsT_scale=w2_plane[:, cols],
+                    rhs=z_codes[:, places].bitcast(FP8X4),
+                    rhs_scale=z_plane[:, places],
+                    start=True,
+                    stop=True,
+                )
+
+        out_rows = out.rearrange("(p t) j -> p t j", t=PACK)
+        window = []
+        for t in range(PACK):
+            row = keep.tile([P, S], F32, name="window%d" % t)
+            window.append(row)
+            if t in VECTOR_GATHERS:
+                nc.scalar.activation(row[:], h_psum[t][:], ACT.Sigmoid)
+            elif t == 1:
+                nc.scalar.copy(row[:], h_psum[t][:])
+            else:
+                nc.vector.tensor_copy(row[:], h_psum[t][:])
+        for t in range(PACK):
+            for half in range(2):
+                places = slice(half * HALF, (half + 1) * HALF)
+                looked_up = window[t][:].indirect(n3_sb[:, half * 16 : (half + 1) * 16])
+                gate = keep.tile([P, HALF], F32, name="gate%d_%d" % (t, half))
+                if t in VECTOR_GATHERS:
+                    nc.vector.tensor_copy(gate[:], looked_up)
+                else:
+                    nc.scalar.activation(gate[:], looked_up, ACT.Sigmoid)
+                res = keep.tile([P, HALF], F32, name="res%d_%d" % (t, half))
+                nc.vector.tensor_tensor(res[:], h_psum[t][:, places], gate[:], ALU.mult)
+                nc.sync.dma_start(out=out_rows[:, t, places], in_=res[:])

@@ -18,24 +18,20 @@ ACT = mybir.ActivationFunctionType
 P = 128
 PACK = 4
 HALF = 256
-W1_SCALAR_COLS = 96
-VECTOR_GATHERS = (0,)
+W1_VECTOR_COLS = 352
+Z_VECTOR_COLS = 384
+VECTOR_GATHERS = (0, 2)
 
 
 def load_weight(nc, pool, w):
-    rows = w.rearrange("(p j) c -> p j c", j=PACK)
-    halves = []
-    for n in range(2):
-        raw = pool.tile([P, PACK, HALF], F32, name="raw%d" % n)
-        nc.sync.dma_start(out=raw[:], in_=rows[:, :, n * HALF : (n + 1) * HALF])
-        halves.append(raw)
-    return halves
+    raw = pool.tile([P, PACK, w.shape[1]], F32, name="raw")
+    nc.sync.dma_start(out=raw[:], in_=w.rearrange("(p j) c -> p j c", j=PACK))
+    return raw
 
 
-def round_and_deal(copy, grouped, halves, c0, c1):
-    raw = halves[c0 // HALF][:, :, c0 % HALF : (c1 - 1) % HALF + 1]
+def round_and_deal(copy, grouped, raw, c0, c1):
     m = slice(c0 // PACK, c1 // PACK)
-    copy(grouped[:, :, m, :].rearrange("p t m j -> p m j t"), raw.rearrange("p j (m t) -> p m j t", t=PACK))
+    copy(grouped[:, :, m, :].rearrange("p t m j -> p m j t"), raw[:, :, c0:c1].rearrange("p j (m t) -> p m j t", t=PACK))
 
 
 def tile_picked_hashfillgate_none_p_kernel(tc, x_words, x_scales, w1, gn, w2, offs, n1, n2, n3, out):
@@ -44,128 +40,143 @@ def tile_picked_hashfillgate_none_p_kernel(tc, x_words, x_scales, w1, gn, w2, of
         keep = ctx.enter_context(tc.tile_pool(name="keep", bufs=1))
         stage = ctx.enter_context(tc.tile_pool(name="stage", bufs=1))
         psum = ctx.enter_context(tc.psum_pool(name="psum", bufs=1))
+        halves = [slice(0, HALF), slice(HALF, S)]
+        list_halves = [slice(0, HALF // 16), slice(HALF // 16, S // 16)]
 
-        scale_table = stage.tile([P, T], U8, align_bytes=64, tag="x_side")
+        scale_table = keep.tile([P, T], U8, align_bytes=64)
         nc.vector.memset(scale_table[:].bitcast(I32), 0)
         warm = keep.tile([P, 8], F32)
         nc.vector.memset(warm[:], 0.0)
-        offs_sb = keep.tile([P, S // 16], U16)
-        nc.sync.dma_start(offs_sb[:], offs)
         warm_out = keep.tile([P, 8], F32)
         nc.scalar.activation(warm_out[:], warm[:], ACT.Sigmoid)
 
+        offs_sb = keep.tile([P, S // 16], U16)
+        nc.sync.dma_start(offs_sb[:], offs)
+        nc.sync.dma_start(out=scale_table[:].bitcast(I32)[0:P:8, :], in_=x_scales[0].bitcast(I32))
         n1_sb = keep.tile([P, W // 16], U16)
         nc.sync.dma_start(n1_sb[:], n1)
-        n2_sb = keep.tile([P, W // 16], U16)
-        nc.sync.dma_start(n2_sb[:], n2)
-        n3_sb = keep.tile([P, S // 16], U16)
-        nc.sync.dma_start(n3_sb[:], n3)
-        gain = keep.tile([P, PACK], F32)
-        nc.sync.dma_start(out=gain[:], in_=gn.rearrange("(p t) o -> p (t o)", t=PACK))
-        scale_rows = x_scales[0].bitcast(I32)
-        for e in range(2):
-            nc.sync.dma_start(out=scale_table[:].bitcast(I32)[e:P:16, :], in_=scale_rows[e:16:2, :])
+        w1_raw = load_weight(nc, stage, w1)
         word_table = keep.tile([P, T], U32, align_bytes=64)
         nc.sync.dma_start(out=word_table[:].bitcast(I32), in_=x_words[0].rearrange("p n t -> p (n t)").bitcast(I32))
-        w1_halves = load_weight(nc, stage, w1)
+        n2_sb = keep.tile([P, W // 16], U16)
+        nc.sync.dma_start(n2_sb[:], n2)
+        gain = keep.tile([P, PACK], F32)
+        nc.sync.dma_start(out=gain[:], in_=gn.rearrange("(p t) o -> p (t o)", t=PACK))
+        n3_sb = keep.tile([P, S // 16], U16)
+        nc.sync.dma_start(n3_sb[:], n3)
 
         picked_scales = keep.tile([P, S], U8, align_bytes=64)
         nc.vector.tensor_copy(picked_scales[:], scale_table[:].indirect(offs_sb[:]))
         x_plane = keep.tile([P, S], U8, align_bytes=64)
         nc.vector.tensor_copy(x_plane[:].bitcast(I32), picked_scales[:].bitcast(I32))
-        for e in range(2):
-            nc.scalar.dma_start(out=x_plane[:].bitcast(I32)[2 + e : P : 32, :], in_=picked_scales[:].bitcast(I32)[16 + e : P : 32, :])
-        x_codes = stage.tile([P, S], U32, align_bytes=64, tag="x_side")
-        nc.vector.tensor_copy(x_codes[:], word_table[:].indirect(offs_sb[:]))
+        for i in range(1, 4):
+            nc.sync.dma_start(out=x_plane[:].bitcast(I32)[i:P:32, :], in_=picked_scales[:].bitcast(I32)[8 * i : P : 32, :])
 
         w1_grouped = keep.tile([P, PACK, P, PACK], BF16, align_bytes=64)
-        round_and_deal(nc.vector.tensor_copy, w1_grouped, w1_halves, 0, HALF)
-        round_and_deal(nc.vector.tensor_copy, w1_grouped, w1_halves, HALF, H - W1_SCALAR_COLS)
-        round_and_deal(nc.scalar.copy, w1_grouped, w1_halves, H - W1_SCALAR_COLS, H)
+        round_and_deal(nc.vector.tensor_copy, w1_grouped, w1_raw, 0, W1_VECTOR_COLS)
+        round_and_deal(nc.scalar.copy, w1_grouped, w1_raw, W1_VECTOR_COLS, H)
         w1_codes = keep.tile([P, H], U32, align_bytes=64)
         w1_plane = keep.tile([P, H], U8, align_bytes=64)
-        order = (1, 0, 3, 2)
+        nc.vector.quantize_mx(
+            out=w1_codes[:].bitcast(FP8X4),
+            scales=w1_plane[:],
+            in_=w1_grouped[:].rearrange("p t m j -> p (t m j)"),
+        )
+
+        x_codes = []
+        for half in range(2):
+            codes = keep.tile([P, HALF], U32, align_bytes=64, name="x_codes%d" % half)
+            nc.vector.tensor_copy(codes[:], word_table[:].indirect(offs_sb[:, list_halves[half]]))
+            x_codes.append(codes)
+
+        order = (3, 0, 1, 2)
+        mate, last = order[0], order[3]
+        y = {}
         y_psum = {}
         for t in order:
             cols = slice(t * P, (t + 1) * P)
-            nc.vector.quantize_mx(
-                out=w1_codes[:, cols].bitcast(FP8X4),
-                scales=w1_plane[:, cols],
-                in_=w1_grouped[:, t, :, :].rearrange("p m j -> p (m j)"),
-            )
-            y_psum[t] = psum.tile([P, S], F32, name="y_psum%d" % t)
-            nc.tensor.matmul_mx(
-                out=y_psum[t][:],
-                lhsT=w1_codes[:, cols].bitcast(FP8X4),
-                lhsT_scale=w1_plane[:, cols],
-                rhs=x_codes[:].bitcast(FP8X4),
-                rhs_scale=x_plane[:],
-                start=True,
-                stop=True,
-            )
-
-        y = {}
-        for t in order:
             y[t] = keep.tile([P, S], F32, name="y%d" % t)
-            nc.scalar.copy(y[t][:], y_psum[t][:])
+            for half in range(2):
+                bank = psum.tile([P, HALF], F32, name="y_psum", tag="bank%d" % (2 * t + half))
+                y_psum[t, half] = bank
+                nc.tensor.matmul_mx(
+                    out=bank[:],
+                    lhsT=w1_codes[:, cols].bitcast(FP8X4),
+                    lhsT_scale=w1_plane[:, cols],
+                    rhs=x_codes[half][:].bitcast(FP8X4),
+                    rhs_scale=x_plane[:, halves[half]],
+                    start=True,
+                    stop=True,
+                )
+                nc.scalar.copy(y[t][:, halves[half]], bank[:])
 
-        last, mate = order[3], order[2]
         z_pair = keep.tile([P, 2 * S], F32)
-        nc.scalar.activation(z_pair[:, :S], y_psum[last][:], ACT.Copy, scale=gain[:, last : last + 1])
+        for half in range(2):
+            nc.scalar.activation(z_pair[:, halves[half]], y_psum[last, half][:], ACT.Copy, scale=gain[:, last : last + 1])
         gain_wide = keep.tile([P, W], F32)
         nc.scalar.activation(gain_wide[:], gain[:, last : last + 1].to_broadcast([P, W]), ACT.Copy)
 
-        w2_halves = load_weight(nc, stage, w2)
+        w2_raw = load_weight(nc, stage, w2)
         w2_grouped = keep.tile([P, PACK, P, PACK], BF16, align_bytes=64)
-        w2_codes = keep.tile([P, N], U32, align_bytes=64)
+        w2_first = keep.tile([P, P], U32, align_bytes=64)
         w2_plane = keep.tile([P, N], U8, align_bytes=64)
-        for n in range(2):
-            round_and_deal(nc.scalar.copy, w2_grouped, w2_halves, n * HALF, (n + 1) * HALF)
+        round_and_deal(nc.scalar.copy, w2_grouped, w2_raw, 0, N)
         nc.vector.quantize_mx(
-            out=w2_codes[:].bitcast(FP8X4),
-            scales=w2_plane[:],
-            in_=w2_grouped[:].rearrange("p t m j -> p (t m j)"),
+            out=w2_first[:].bitcast(FP8X4),
+            scales=w2_plane[:, :P],
+            in_=w2_grouped[:, 0, :, :].rearrange("p m j -> p (m j)"),
         )
 
-        z_grouped = keep.tile([P, S, PACK], BF16, align_bytes=64)
-        for t in order:
-            pa = keep.tile([P, W], F32, name="pa%d" % t)
-            pb = keep.tile([P, W], F32, name="pb%d" % t)
-            ra = keep.tile([P, W], F32, name="ra%d" % t)
-            nc.vector.tensor_copy(pa[:], y[t][:].indirect(n1_sb[:]))
-            nc.vector.tensor_copy(pb[:], y[t][:].indirect(n2_sb[:]))
-            nc.vector.tensor_tensor(ra[:], pa[:], pb[:], ALU.max)
+        z_grouped = stage.tile([P, S, PACK], BF16, align_bytes=64, tag="z_then_w2")
+        pa = keep.tile([P, PACK, W], F32)
+        pb = keep.tile([P, PACK, W], F32)
+        ra = keep.tile([P, PACK, W], F32)
+        for n, t in enumerate(order):
+            nc.vector.tensor_copy(pa[:, n, :], y[t][:].indirect(n1_sb[:]))
+            nc.vector.tensor_copy(pb[:, n, :], y[t][:].indirect(n2_sb[:]))
+            if n % 2 == 1:
+                nc.vector.tensor_tensor(ra[:, n - 1 : n + 1, :], pa[:, n - 1 : n + 1, :], pb[:, n - 1 : n + 1, :], ALU.max)
+        for n, t in enumerate(order):
             if t == last:
-                nc.vector.tensor_tensor(z_pair[:].indirect(n1_sb[:]), ra[:], gain_wide[:], ALU.mult)
+                nc.vector.tensor_tensor(z_pair[:].indirect(n1_sb[:]), ra[:, n, :], gain_wide[:], ALU.mult)
             else:
-                nc.vector.tensor_copy(y[t][:].indirect(n1_sb[:]), ra[:])
+                nc.vector.tensor_copy(y[t][:].indirect(n1_sb[:]), ra[:, n, :])
                 dst = z_pair[:, S:] if t == mate else z_grouped[:, :, t]
                 nc.scalar.activation(dst, y[t][:], ACT.Copy, scale=gain[:, t : t + 1])
 
         src = z_pair[:].rearrange("p (e c) -> p c e", e=2)
         z_codes = keep.tile([P, S], U32, align_bytes=64)
         z_plane = keep.tile([P, S], U8, align_bytes=64)
-        for half, copy in enumerate((nc.vector.tensor_copy, nc.scalar.copy)):
-            places = slice(half * HALF, (half + 1) * HALF)
+        for copy, places in (
+            (nc.vector.tensor_copy, halves[0]),
+            (nc.vector.tensor_copy, slice(HALF, Z_VECTOR_COLS)),
+            (nc.scalar.copy, slice(Z_VECTOR_COLS, S)),
+        ):
             copy(z_grouped[:, places, last : mate + 1], src[:, places, :])
-        for half in range(2):
-            places = slice(half * HALF, (half + 1) * HALF)
+        for places in halves:
             nc.vector.quantize_mx(
                 out=z_codes[:, places].bitcast(FP8X4),
                 scales=z_plane[:, places],
                 in_=z_grouped[:, places, :].rearrange("p c t -> p (c t)"),
             )
 
-        h_psum = []
+        w2_rest = stage.tile([P, N - P], U32, align_bytes=64, tag="z_then_w2")
+        for t0, t1 in ((1, 2), (2, 4)):
+            nc.vector.quantize_mx(
+                out=w2_rest[:, (t0 - 1) * P : (t1 - 1) * P].bitcast(FP8X4),
+                scales=w2_plane[:, t0 * P : t1 * P],
+                in_=w2_grouped[:, t0:t1, :, :].rearrange("p t m j -> p (t m j)"),
+            )
+        w2_codes = [w2_first[:]] + [w2_rest[:, t * P : (t + 1) * P] for t in range(PACK - 1)]
+
+        h_psum = {}
         for t in range(PACK):
             cols = slice(t * P, (t + 1) * P)
-            bank = psum.tile([P, S], F32, name="h_psum%d" % t)
-            h_psum.append(bank)
-            for half in range(2):
-                places = slice(half * HALF, (half + 1) * HALF)
+            for half, places in enumerate(halves):
+                h_psum[t, half] = psum.tile([P, HALF], F32, name="h_psum", tag="bank%d" % (2 * t + half))
                 nc.tensor.matmul_mx(
-                    out=bank[:, places],
-                    lhsT=w2_codes[:, cols].bitcast(FP8X4),
+                    out=h_psum[t, half][:],
+                    lhsT=w2_codes[t].bitcast(FP8X4),
                     lhsT_scale=w2_plane[:, cols],
                     rhs=z_codes[:, places].bitcast(FP8X4),
                     rhs_scale=z_plane[:, places],
@@ -178,21 +189,24 @@ def tile_picked_hashfillgate_none_p_kernel(tc, x_words, x_scales, w1, gn, w2, of
         for t in range(PACK):
             row = keep.tile([P, S], F32, name="window%d" % t)
             window.append(row)
-            if t in VECTOR_GATHERS:
-                nc.scalar.activation(row[:], h_psum[t][:], ACT.Sigmoid)
-            elif t == 1:
-                nc.scalar.copy(row[:], h_psum[t][:])
-            else:
-                nc.vector.tensor_copy(row[:], h_psum[t][:])
-        for t in range(PACK):
-            for half in range(2):
-                places = slice(half * HALF, (half + 1) * HALF)
-                looked_up = window[t][:].indirect(n3_sb[:, half * 16 : (half + 1) * 16])
-                gate = keep.tile([P, HALF], F32, name="gate%d_%d" % (t, half))
+            for half, places in enumerate(halves):
                 if t in VECTOR_GATHERS:
-                    nc.vector.tensor_copy(gate[:], looked_up)
+                    nc.scalar.activation(row[:, places], h_psum[t, half][:], ACT.Sigmoid)
+                elif (t, half) in ((3, 0), (3, 1)):
+                    nc.vector.tensor_copy(row[:, places], h_psum[t, half][:])
                 else:
-                    nc.scalar.activation(gate[:], looked_up, ACT.Sigmoid)
-                res = keep.tile([P, HALF], F32, name="res%d_%d" % (t, half))
-                nc.vector.tensor_tensor(res[:], h_psum[t][:, places], gate[:], ALU.mult)
-                nc.sync.dma_start(out=out_rows[:, t, places], in_=res[:])
+                    nc.scalar.copy(row[:, places], h_psum[t, half][:])
+        for t, c0, c1 in ((0, 0, 256), (0, 256, 512), (1, 0, 256), (1, 256, 512), (2, 0, 256), (3, 0, 256), (2, 256, 512), (3, 256, 384), (3, 384, 512)):
+            places = slice(c0, c1)
+            looked_up = window[t][:].indirect(n3_sb[:, c0 // 16 : c1 // 16])
+            gate = keep.tile([P, c1 - c0], F32, name="gate%d_%d" % (t, c0))
+            if t in VECTOR_GATHERS:
+                nc.vector.tensor_copy(gate[:], looked_up)
+            else:
+                nc.scalar.activation(gate[:], looked_up, ACT.Sigmoid)
+            res = keep.tile([P, c1 - c0], F32, name="res%d_%d" % (t, c0))
+            if (t, c0) in ((1, 0), (1, 256), (3, 0), (3, 256), (3, 384)):
+                nc.gpsimd.tensor_tensor(res[:], window[t][:, places], gate[:], ALU.mult)
+            else:
+                nc.vector.tensor_tensor(res[:], h_psum[t, c0 // HALF][:, c0 % HALF : (c1 - 1) % HALF + 1], gate[:], ALU.mult)
+            nc.sync.dma_start(out=out_rows[:, t, places], in_=res[:])

@@ -50,14 +50,17 @@ def tile_picked_hashfillgate_none_p_kernel(tc, x_words, x_scales, w1, gn, w2, of
         warm_out = keep.tile([P, 8], F32)
         nc.scalar.activation(warm_out[:], warm[:], ACT.Sigmoid)
 
+        w1_rows = w1.rearrange("(p j) c -> p j c", j=PACK)
+        w1_raw = stage.tile([P, PACK, H], F32, name="raw")
+        nc.sync.dma_start(out=w1_raw[:, :2, :], in_=w1_rows[:, :2, :])
         offs_sb = keep.tile([P, S // 16], U16)
         nc.sync.dma_start(offs_sb[:], offs)
         nc.sync.dma_start(out=scale_table[:].bitcast(I32)[0:P:8, :], in_=x_scales[0].bitcast(I32))
+        nc.sync.dma_start(out=w1_raw[:, 2:, :], in_=w1_rows[:, 2:, :])
+        word_table = stage.tile([P, T], U32, align_bytes=64, tag="words_then_w1")
+        nc.sync.dma_start(out=word_table[:].bitcast(I32), in_=x_words[0].rearrange("p n t -> p (n t)").bitcast(I32))
         n1_sb = keep.tile([P, W // 16], U16)
         nc.sync.dma_start(n1_sb[:], n1)
-        w1_raw = load_weight(nc, stage, w1)
-        word_table = keep.tile([P, T], U32, align_bytes=64)
-        nc.sync.dma_start(out=word_table[:].bitcast(I32), in_=x_words[0].rearrange("p n t -> p (n t)").bitcast(I32))
         n2_sb = keep.tile([P, W // 16], U16)
         nc.sync.dma_start(n2_sb[:], n2)
         gain = keep.tile([P, PACK], F32)
@@ -75,12 +78,12 @@ def tile_picked_hashfillgate_none_p_kernel(tc, x_words, x_scales, w1, gn, w2, of
         w1_grouped = keep.tile([P, PACK, P, PACK], BF16, align_bytes=64)
         round_and_deal(nc.vector.tensor_copy, w1_grouped, w1_raw, 0, W1_VECTOR_COLS)
         round_and_deal(nc.scalar.copy, w1_grouped, w1_raw, W1_VECTOR_COLS, H)
-        w1_codes = keep.tile([P, H], U32, align_bytes=64)
+        w1_first = keep.tile([P, P], U32, align_bytes=64)
         w1_plane = keep.tile([P, H], U8, align_bytes=64)
         nc.vector.quantize_mx(
-            out=w1_codes[:].bitcast(FP8X4),
-            scales=w1_plane[:],
-            in_=w1_grouped[:].rearrange("p t m j -> p (t m j)"),
+            out=w1_first[:].bitcast(FP8X4),
+            scales=w1_plane[:, 3 * P :],
+            in_=w1_grouped[:, 3, :, :].rearrange("p m j -> p (m j)"),
         )
 
         x_codes = []
@@ -88,6 +91,15 @@ def tile_picked_hashfillgate_none_p_kernel(tc, x_words, x_scales, w1, gn, w2, of
             codes = keep.tile([P, HALF], U32, align_bytes=64, name="x_codes%d" % half)
             nc.vector.tensor_copy(codes[:], word_table[:].indirect(offs_sb[:, list_halves[half]]))
             x_codes.append(codes)
+
+        w1_rest = stage.tile([P, H - P], U32, align_bytes=64, tag="words_then_w1")
+        for t0, t1 in ((0, 1), (1, 3)):
+            nc.vector.quantize_mx(
+                out=w1_rest[:, t0 * P : t1 * P].bitcast(FP8X4),
+                scales=w1_plane[:, t0 * P : t1 * P],
+                in_=w1_grouped[:, t0:t1, :, :].rearrange("p t m j -> p (t m j)"),
+            )
+        w1_codes = [w1_rest[:, t * P : (t + 1) * P] for t in range(PACK - 1)] + [w1_first[:]]
 
         order = (3, 0, 1, 2)
         mate, last = order[0], order[3]
@@ -101,7 +113,7 @@ def tile_picked_hashfillgate_none_p_kernel(tc, x_words, x_scales, w1, gn, w2, of
                 y_psum[t, half] = bank
                 nc.tensor.matmul_mx(
                     out=bank[:],
-                    lhsT=w1_codes[:, cols].bitcast(FP8X4),
+                    lhsT=w1_codes[t].bitcast(FP8X4),
                     lhsT_scale=w1_plane[:, cols],
                     rhs=x_codes[half][:].bitcast(FP8X4),
                     rhs_scale=x_plane[:, halves[half]],

from contextlib import ExitStack

import concourse.mybir as mybir

K, T, S, H, N, W = 512, 2048, 512, 512, 512, 256
FLOPS = 2 * K * H * S + 2 * H * N * S

F32 = mybir.dt.float32
BF16 = mybir.dt.bfloat16
I32 = mybir.dt.int32
U32 = mybir.dt.uint32
U16 = mybir.dt.uint16
U8 = mybir.dt.uint8
FP8X4 = mybir.dt.float8_e4m3fn_x4
ALU = mybir.AluOpType
ACT = mybir.ActivationFunctionType

P = 128
PACK = 4
HALF = 256
W1_VECTOR_COLS = 352
Z_VECTOR_COLS = 384
VECTOR_GATHERS = (0, 2)


def load_weight(nc, pool, w):
    raw = pool.tile([P, PACK, w.shape[1]], F32, name="raw")
    nc.sync.dma_start(out=raw[:], in_=w.rearrange("(p j) c -> p j c", j=PACK))
    return raw


def round_and_deal(copy, grouped, raw, c0, c1):
    m = slice(c0 // PACK, c1 // PACK)
    copy(grouped[:, :, m, :].rearrange("p t m j -> p m j t"), raw[:, :, c0:c1].rearrange("p j (m t) -> p m j t", t=PACK))


def tile_picked_hashfillgate_none_p_kernel(tc, x_words, x_scales, w1, gn, w2, offs, n1, n2, n3, out):
    nc = tc.nc
    with ExitStack() as ctx:
        keep = ctx.enter_context(tc.tile_pool(name="keep", bufs=1))
        stage = ctx.enter_context(tc.tile_pool(name="stage", bufs=1))
        psum = ctx.enter_context(tc.psum_pool(name="psum", bufs=1))
        halves = [slice(0, HALF), slice(HALF, S)]
        list_halves = [slice(0, HALF // 16), slice(HALF // 16, S // 16)]

        scale_table = keep.tile([P, T], U8, align_bytes=64)
        nc.vector.memset(scale_table[:].bitcast(I32), 0)
        warm = keep.tile([P, 8], F32)
        nc.vector.memset(warm[:], 0.0)
        warm_out = keep.tile([P, 8], F32)
        nc.scalar.activation(warm_out[:], warm[:], ACT.Sigmoid)

        w1_rows = w1.rearrange("(p j) c -> p j c", j=PACK)
        w1_raw = stage.tile([P, PACK, H], F32, name="raw")
        nc.sync.dma_start(out=w1_raw[:, :2, :], in_=w1_rows[:, :2, :])
        offs_sb = keep.tile([P, S // 16], U16)
        nc.sync.dma_start(offs_sb[:], offs)
        nc.sync.dma_start(out=scale_table[:].bitcast(I32)[0:P:8, :], in_=x_scales[0].bitcast(I32))
        nc.sync.dma_start(out=w1_raw[:, 2:, :], in_=w1_rows[:, 2:, :])
        word_table = stage.tile([P, T], U32, align_bytes=64, tag="words_then_w1")
        nc.sync.dma_start(out=word_table[:].bitcast(I32), in_=x_words[0].rearrange("p n t -> p (n t)").bitcast(I32))
        n1_sb = keep.tile([P, W // 16], U16)
        nc.sync.dma_start(n1_sb[:], n1)
        n2_sb = keep.tile([P, W // 16], U16)
        nc.sync.dma_start(n2_sb[:], n2)
        gain = keep.tile([P, PACK], F32)
        nc.sync.dma_start(out=gain[:], in_=gn.rearrange("(p t) o -> p (t o)", t=PACK))
        n3_sb = keep.tile([P, S // 16], U16)
        nc.sync.dma_start(n3_sb[:], n3)

        picked_scales = keep.tile([P, S], U8, align_bytes=64)
        nc.vector.tensor_copy(picked_scales[:], scale_table[:].indirect(offs_sb[:]))
        x_plane = keep.tile([P, S], U8, align_bytes=64)
        nc.vector.tensor_copy(x_plane[:].bitcast(I32), picked_scales[:].bitcast(I32))
        for i in range(1, 4):
            nc.sync.dma_start(out=x_plane[:].bitcast(I32)[i:P:32, :], in_=picked_scales[:].bitcast(I32)[8 * i : P : 32, :])

        w1_grouped = keep.tile([P, PACK, P, PACK], BF16, align_bytes=64)
        round_and_deal(nc.vector.tensor_copy, w1_grouped, w1_raw, 0, W1_VECTOR_COLS)
        round_and_deal(nc.scalar.copy, w1_grouped, w1_raw, W1_VECTOR_COLS, H)
        w1_first = keep.tile([P, P], U32, align_bytes=64)
        w1_plane = keep.tile([P, H], U8, align_bytes=64)
        nc.vector.quantize_mx(
            out=w1_first[:].bitcast(FP8X4),
            scales=w1_plane[:, 3 * P :],
            in_=w1_grouped[:, 3, :, :].rearrange("p m j -> p (m j)"),
        )

        x_codes = []
        for half in range(2):
            codes = keep.tile([P, HALF], U32, align_bytes=64, name="x_codes%d" % half)
            nc.vector.tensor_copy(codes[:], word_table[:].indirect(offs_sb[:, list_halves[half]]))
            x_codes.append(codes)

        w1_rest = stage.tile([P, H - P], U32, align_bytes=64, tag="words_then_w1")
        for t0, t1 in ((0, 1), (1, 3)):
            nc.vector.quantize_mx(
                out=w1_rest[:, t0 * P : t1 * P].bitcast(FP8X4),
                scales=w1_plane[:, t0 * P : t1 * P],
                in_=w1_grouped[:, t0:t1, :, :].rearrange("p t m j -> p (t m j)"),
            )
        w1_codes = [w1_rest[:, t * P : (t + 1) * P] for t in range(PACK - 1)] + [w1_first[:]]

        order = (3, 0, 1, 2)
        mate, last = order[0], order[3]
        y = {}
        y_psum = {}
        for t in order:
            cols = slice(t * P, (t + 1) * P)
            y[t] = keep.tile([P, S], F32, name="y%d" % t)
            for half in range(2):
                bank = psum.tile([P, HALF], F32, name="y_psum", tag="bank%d" % (2 * t + half))
                y_psum[t, half] = bank
                nc.tensor.matmul_mx(
                    out=bank[:],
                    lhsT=w1_codes[t].bitcast(FP8X4),
                    lhsT_scale=w1_plane[:, cols],
                    rhs=x_codes[half][:].bitcast(FP8X4),
                    rhs_scale=x_plane[:, halves[half]],
                    start=True,
                    stop=True,
                )
                nc.scalar.copy(y[t][:, halves[half]], bank[:])

        z_pair = keep.tile([P, 2 * S], F32)
        for half in range(2):
            nc.scalar.activation(z_pair[:, halves[half]], y_psum[last, half][:], ACT.Copy, scale=gain[:, last : last + 1])
        gain_wide = keep.tile([P, W], F32)
        nc.scalar.activation(gain_wide[:], gain[:, last : last + 1].to_broadcast([P, W]), ACT.Copy)

        w2_raw = load_weight(nc, stage, w2)
        w2_grouped = keep.tile([P, PACK, P, PACK], BF16, align_bytes=64)
        w2_first = keep.tile([P, P], U32, align_bytes=64)
        w2_plane = keep.tile([P, N], U8, align_bytes=64)
        round_and_deal(nc.scalar.copy, w2_grouped, w2_raw, 0, N)
        nc.vector.quantize_mx(
            out=w2_first[:].bitcast(FP8X4),
            scales=w2_plane[:, :P],
            in_=w2_grouped[:, 0, :, :].rearrange("p m j -> p (m j)"),
        )

        z_grouped = stage.tile([P, S, PACK], BF16, align_bytes=64, tag="z_then_w2")
        pa = keep.tile([P, PACK, W], F32)
        pb = keep.tile([P, PACK, W], F32)
        ra = keep.tile([P, PACK, W], F32)
        for n, t in enumerate(order):
            nc.vector.tensor_copy(pa[:, n, :], y[t][:].indirect(n1_sb[:]))
            nc.vector.tensor_copy(pb[:, n, :], y[t][:].indirect(n2_sb[:]))
            if n % 2 == 1:
                nc.vector.tensor_tensor(ra[:, n - 1 : n + 1, :], pa[:, n - 1 : n + 1, :], pb[:, n - 1 : n + 1, :], ALU.max)
        for n, t in enumerate(order):
            if t == last:
                nc.vector.tensor_tensor(z_pair[:].indirect(n1_sb[:]), ra[:, n, :], gain_wide[:], ALU.mult)
            else:
                nc.vector.tensor_copy(y[t][:].indirect(n1_sb[:]), ra[:, n, :])
                dst = z_pair[:, S:] if t == mate else z_grouped[:, :, t]
                nc.scalar.activation(dst, y[t][:], ACT.Copy, scale=gain[:, t : t + 1])

        src = z_pair[:].rearrange("p (e c) -> p c e", e=2)
        z_codes = keep.tile([P, S], U32, align_bytes=64)
        z_plane = keep.tile([P, S], U8, align_bytes=64)
        for copy, places in (
            (nc.vector.tensor_copy, halves[0]),
            (nc.vector.tensor_copy, slice(HALF, Z_VECTOR_COLS)),
            (nc.scalar.copy, slice(Z_VECTOR_COLS, S)),
        ):
            copy(z_grouped[:, places, last : mate + 1], src[:, places, :])
        for places in halves:
            nc.vector.quantize_mx(
                out=z_codes[:, places].bitcast(FP8X4),
                scales=z_plane[:, places],
                in_=z_grouped[:, places, :].rearrange("p c t -> p (c t)"),
            )

        w2_rest = stage.tile([P, N - P], U32, align_bytes=64, tag="z_then_w2")
        for t0, t1 in ((1, 2), (2, 4)):
            nc.vector.quantize_mx(
                out=w2_rest[:, (t0 - 1) * P : (t1 - 1) * P].bitcast(FP8X4),
                scales=w2_plane[:, t0 * P : t1 * P],
                in_=w2_grouped[:, t0:t1, :, :].rearrange("p t m j -> p (t m j)"),
            )
        w2_codes = [w2_first[:]] + [w2_rest[:, t * P : (t + 1) * P] for t in range(PACK - 1)]

        h_psum = {}
        for t in range(PACK):
            cols = slice(t * P, (t + 1) * P)
            for half, places in enumerate(halves):
                h_psum[t, half] = psum.tile([P, HALF], F32, name="h_psum", tag="bank%d" % (2 * t + half))
                nc.tensor.matmul_mx(
                    out=h_psum[t, half][:],
                    lhsT=w2_codes[t].bitcast(FP8X4),
                    lhsT_scale=w2_plane[:, cols],
                    rhs=z_codes[:, places].bitcast(FP8X4),
                    rhs_scale=z_plane[:, places],
                    start=True,
                    stop=True,
                )

        out_rows = out.rearrange("(p t) j -> p t j", t=PACK)
        window = []
        for t in range(PACK):
            row = keep.tile([P, S], F32, name="window%d" % t)
            window.append(row)
            for half, places in enumerate(halves):
                if t in VECTOR_GATHERS:
                    nc.scalar.activation(row[:, places], h_psum[t, half][:], ACT.Sigmoid)
                elif (t, half) in ((3, 0), (3, 1)):
                    nc.vector.tensor_copy(row[:, places], h_psum[t, half][:])
                else:
                    nc.scalar.copy(row[:, places], h_psum[t, half][:])
        for t, c0, c1 in ((0, 0, 256), (0, 256, 512), (1, 0, 256), (1, 256, 512), (2, 0, 256), (3, 0, 256), (2, 256, 512), (3, 256, 384), (3, 384, 512)):
            places = slice(c0, c1)
            looked_up = window[t][:].indirect(n3_sb[:, c0 // 16 : c1 // 16])
            gate = keep.tile([P, c1 - c0], F32, name="gate%d_%d" % (t, c0))
            if t in VECTOR_GATHERS:
                nc.vector.tensor_copy(gate[:], looked_up)
            else:
                nc.scalar.activation(gate[:], looked_up, ACT.Sigmoid)
            res = keep.tile([P, c1 - c0], F32, name="res%d_%d" % (t, c0))
            if (t, c0) in ((1, 0), (1, 256), (3, 0), (3, 256), (3, 384)):
                nc.gpsimd.tensor_tensor(res[:], window[t][:, places], gate[:], ALU.mult)
            else:
                nc.vector.tensor_tensor(res[:], h_psum[t, c0 // HALF][:, c0 % HALF : (c1 - 1) % HALF + 1], gate[:], ALU.mult)
            nc.sync.dma_start(out=out_rows[:, t, places], in_=res[:])
